import numpy as np
import ml_dtypes


def mxq(x, axis, fmt="e4m3"):
    dtype, down = {"e4m3": (ml_dtypes.float8_e4m3fn, 7), "e5m2": (ml_dtypes.float8_e5m2, 14)}[fmt]
    v = np.moveaxis(np.asarray(x, np.float32).astype(ml_dtypes.bfloat16).astype(np.float64), axis, -1)
    blocks = v.reshape(v.shape[:-1] + (-1, 32))
    amax = np.abs(blocks).max(-1, keepdims=True)
    byte = np.maximum(np.where(amax > 0, np.frexp(amax)[1] - 1 + 127, 0) - down, 1)
    scale = np.exp2(byte - 127.0)
    codes = (blocks / scale).astype(np.float32).astype(dtype).astype(np.float64)
    return np.moveaxis((codes * scale).reshape(v.shape), -1, axis)


WIDE = False


def mx_kscale(k):
    if not WIDE:
        return np.ones(k)
    levels = np.array([10, -10, 5, -5, 0])
    if k % 512:
        return np.exp2(np.random.permutation(np.resize(levels, k // 32))).repeat(32)
    a = np.empty((k // 512, 16))
    for p in range(k // 512):
        a[p, :8] = np.random.permutation(np.resize(levels, 8))
        for g in range(8):
            far = levels[np.abs(levels - a[p, g]) >= 10]
            a[p, g + 8] = far[np.random.randint(len(far))]
    return np.exp2(a.ravel()).repeat(32)


def f64(x):
    return np.asarray(x).astype(np.float64)


def striped(idx):
    return np.tile(idx.reshape(-1, 16).T, (8, 1)).astype(np.uint16)


def unstriped(offs):
    return offs[:16].T.reshape(-1).astype(np.int64)


E2M1 = np.array([0.0, 0.5, 1.0, 1.5, 2.0, 3.0, 4.0, 6.0, -0.0, -0.5, -1.0, -1.5, -2.0, -3.0, -4.0, -6.0])


def pack_weight(w, fmt):
    k, n = w.shape
    w = f64(np.asarray(w, np.float32).astype(ml_dtypes.bfloat16)).reshape(k // 32, 32, n)
    amax = np.abs(w).max(1)
    if fmt == "e4m3":
        byte = np.frexp(amax)[1] - 1 + 127 - 7
    else:
        mant, ex = np.frexp(amax / 6.0)
        byte = np.where(mant > 0.5, ex, ex - 1) + 127
    byte = np.clip(np.where(amax > 0, byte, 1), 1, 254)
    scaled = (w * np.exp2(127.0 - byte)[:, None, :]).reshape(k, n).astype(np.float32)
    by_word = np.ascontiguousarray(scaled.reshape(k // 512, 128, 4, n).transpose(0, 1, 3, 2))
    if fmt == "e4m3":
        words = by_word.astype(ml_dtypes.float8_e4m3fn).view(np.uint8)
    else:
        c = by_word.astype(ml_dtypes.float4_e2m1fn).view(np.uint8) & 0xF
        words = (c[..., 0::2] | (c[..., 1::2] << 4)).reshape(k // 512, 128, 2 * n)
    return np.ascontiguousarray(words), np.ascontiguousarray(byte.astype(np.uint8).reshape(k // 512, 16, n))


def unpack_weight(words, scales, fmt):
    g, _, n = scales.shape
    words = np.ascontiguousarray(words).reshape(g, 128, n, -1)
    if fmt == "e4m3":
        vals = words.view(ml_dtypes.float8_e4m3fn).astype(np.float64)
    else:
        nib = np.empty((g, 128, n, 4), np.uint8)
        nib[..., 0::2] = words & 0xF
        nib[..., 1::2] = words >> 4
        vals = E2M1[nib]
    vals = vals * np.repeat(np.exp2(scales.astype(np.float64) - 127.0), 8, axis=1)[..., None]
    return vals.transpose(0, 1, 3, 2).reshape(g * 512, n)


def gelu(v):
    return 0.5 * v * (1.0 + np.tanh(np.sqrt(2.0 / np.pi) * (v + 0.044715 * v**3)))


K, H, T, S, T2, P = 1024, 1024, 2048, 512, 1024, 512

def setup_inputs():
    n = np.random.standard_normal
    s = mx_kscale(K)[:, None]
    u = mx_kscale(H)[:, None]
    d = {}
    beat = np.sign(n((K, 1)))
    v = 0.8 * n((K, T)) + beat * np.random.uniform(-1.0, 1.0, (1, T))
    d["tab_words"], d["tab_scales"] = pack_weight(v * s, "e4m3")
    rate = np.sign(n((1, H))) * np.random.uniform(1.4, 2.1, (1, H))
    w1 = 0.15 * n((K, H)) / K ** 0.5 + beat * rate / K
    d["w1"] = (w1 / s).astype(np.float32)
    w4 = n((K, H)) / K ** 0.5 * np.exp(0.3 * n((1, H)))
    d["w4_words"], d["w4_scales"] = pack_weight(w4 * u.T / s, "e2m1")
    d["wgs"] = np.exp(0.3 * n((128, S))).astype(np.float32)
    d["page0"] = (n((H, T2)) * u).astype(np.float32)
    d["anchor"] = (np.random.uniform(0.5, 1.5, H) / H ** 0.5 / u[:, 0] ** 2).astype(np.float32)
    d["slot"] = np.exp(0.4 * n(T2)).astype(np.float32)
    d["offs"] = striped(np.random.permutation(T)[:S])
    d["offs2"] = striped(np.random.permutation(T2)[:S])
    d["offs3"] = striped(np.random.permutation(T2)[:P])
    return d

def reference(tab_words, tab_scales, w1, w4_words, w4_scales, wgs, page0, anchor, slot, offs, offs2, offs3):
    v = unpack_weight(tab_words, tab_scales, "e4m3")[:, unstriped(offs)]
    w4 = unpack_weight(w4_words, w4_scales, "e2m1")
    phase = mxq(f64(w1), 0, "e4m3").T @ v
    lift = w4.T @ v
    h = lift * (np.sin(phase) + np.cos(phase))
    page = f64(page0).copy()
    page[:, unstriped(offs2)] = np.tile(f64(wgs), (H // 128, 1)) * h
    x = np.abs(page[:, unstriped(offs3)]) * f64(anchor)[:, None]
    e = mxq(page, 0, "e4m3").T @ mxq(x, 0, "e4m3")
    return e * f64(slot)[:, None]

@@ -1,0 +1,335 @@
+import math
+from contextlib import ExitStack
+
+import concourse.mybir as mybir
+
+K, H, T, S, T2, PA = 1024, 1024, 2048, 512, 1024, 512
+FLOPS = 2 * (2 * K * H * S + H * T2 * PA)
+
+F32 = mybir.dt.float32
+BF16 = mybir.dt.bfloat16
+I32 = mybir.dt.int32
+U32 = mybir.dt.uint32
+U16 = mybir.dt.uint16
+U8 = mybir.dt.uint8
+E4M3 = mybir.dt.float8_e4m3fn_x4
+E2M1 = mybir.dt.float4_e2m1fn_x4
+ALU = mybir.AluOpType
+ACT = mybir.ActivationFunctionType
+
+P = 128
+PACK = 4
+KP = P * PACK
+PASSES = K // KP
+GROUPS = H // KP
+TILES = GROUPS * PACK
+HALF = KP // 2
+CHUNK = 256
+CHUNKS = T2 // CHUNK
+
+
+def tile_list_firework_cue_anchors_kernel(
+    tc, tab_words, tab_scales, w1, w4_words, w4_scales, wgs, page0, anchor, slot, offs, offs2, offs3, out
+):
+    nc = tc.nc
+    with ExitStack() as ctx:
+        lists = ctx.enter_context(tc.tile_pool(name="lists", bufs=1))
+        keep = ctx.enter_context(tc.tile_pool(name="keep", bufs=1))
+        ring = ctx.enter_context(tc.tile_pool(name="ring", bufs=2))
+        psum = ctx.enter_context(tc.psum_pool(name="psum", bufs=1))
+
+        def held(name, shape, dtype):
+            return keep.tile(shape, dtype, name=name, align_bytes=64)
+
+        def bank(b):
+            return psum.tile([P, KP], F32, name="bank%d" % b)
+
+        tab_sc = held("tab_sc", [P, PASSES * T], U8)
+        w4_sc = held("w4_sc", [P, PASSES * H], U8)
+        zero = held("zero", [P, 1], F32)
+        nc.vector.memset(tab_sc[:].bitcast(I32), 0)
+        nc.vector.memset(w4_sc[:].bitcast(I32), 0)
+        nc.vector.memset(zero[:], 0.0)
+        sin45 = held("sin45", [P, 1], F32)
+        root2 = held("root2", [P, 1], F32)
+        nc.scalar.activation(sin45[:], zero[:], ACT.Sin, bias=math.pi / 4)
+        nc.vector.reciprocal(root2[:], sin45[:])
+
+        idx = lists.tile([P, S // 16], U16, name="idx")
+        idx2 = lists.tile([P, S // 16], U16, name="idx2")
+        idx3 = lists.tile([P, PA // 16], U16, name="idx3")
+        tab_w = [held("tab_w%d" % a, [P, T], U32) for a in range(PASSES)]
+        w1_raw = {}
+        w4_w = {}
+        page = {}
+
+        def load_w1(g, a, u):
+            w1_raw[g, a, u] = held("w1_raw%d%d%d" % (g, a, u), [P, PACK, HALF], F32)
+            rows = w1[a * KP : (a + 1) * KP, g * KP + u * HALF : g * KP + (u + 1) * HALF]
+            nc.sync.dma_start(out=w1_raw[g, a, u][:], in_=rows.rearrange("(p j) c -> p j c", j=PACK))
+
+        def load_w4(g):
+            w4_w[g] = held("w4_w%d" % g, [P, PASSES * 2 * KP], U8)
+            nc.sync.dma_start(
+                out=w4_w[g][:].bitcast(I32).rearrange("p (a n) -> p a n", a=PASSES),
+                in_=w4_words[:, :, 2 * KP * g : 2 * KP * (g + 1)].bitcast(I32).rearrange("a p n -> p a n"),
+            )
+
+        def load_page(i):
+            g, t = divmod(i, PACK)
+            page[i] = held("page%d" % i, [P, T2], F32)
+            rows = page0[g * KP : (g + 1) * KP, :].rearrange("(p t) m -> p t m", t=PACK)
+            nc.sync.dma_start(out=page[i][:], in_=rows[:, t, :])
+
+        def load_scales(queue, dst, src):
+            for q in range(4):
+                queue.dma_start(
+                    out=dst[32 * q : 32 * q + 4, :].bitcast(I32).rearrange("r (a n) -> r a n", a=PASSES),
+                    in_=src[:, 4 * q : 4 * q + 4, :].bitcast(I32).rearrange("a r n -> r a n"),
+                )
+
+        wgs_rows = wgs.rearrange("(q t) j -> q t j", t=PACK)
+        wg_first = held("wg_first", [P, 1, S], F32)
+        wg_rest = held("wg_rest", [P, PACK - 1, S], F32)
+
+        def wg(t):
+            return wg_first[:, 0, :] if t == 0 else wg_rest[:, t - 1, :]
+
+        nc.sync.dma_start(out=idx[:], in_=offs)
+        for a in range(PASSES):
+            nc.sync.dma_start(
+                out=tab_w[a][:].bitcast(I32), in_=tab_words[a].rearrange("p n t -> p (n t)").bitcast(I32)
+            )
+        load_w4(0)
+        load_scales(nc.scalar, tab_sc, tab_scales)
+        load_scales(nc.gpsimd, w4_sc, w4_scales)
+        for a in range(PASSES):
+            for u in range(2):
+                load_w1(0, a, u)
+        load_w4(1)
+        for q in range(4):
+            nc.sync.dma_start(out=wg_first[32 * q : 32 * (q + 1)], in_=wgs_rows[:, 0:1, :])
+        nc.sync.dma_start(out=idx2[:], in_=offs2)
+        load_page(0)
+        nc.sync.dma_start(out=idx3[:], in_=offs3)
+        for q in range(4):
+            nc.sync.dma_start(out=wg_rest[32 * q : 32 * (q + 1)], in_=wgs_rows[:, 1:PACK, :])
+        anc = held("anc", [P, GROUPS, PACK], F32)
+        nc.sync.dma_start(out=anc[:], in_=anchor.rearrange("(g p t) -> p g t", g=GROUPS, t=PACK))
+        load_page(1)
+        for a in range(PASSES):
+            for u in range(2):
+                load_w1(1, a, u)
+        for i in range(2, TILES):
+            load_page(i)
+
+        slot_c = held("slot_c", [P, T2 // P], F32)
+        with nc.allow_non_contiguous_dma(reason="one factor a partition"):
+            nc.sync.dma_start(out=slot_c[:], in_=slot.rearrange("(c p) -> p c", p=P))
+        nonneg = held("nonneg", [P, GROUPS, PACK], F32)
+        sgn = held("sgn", [P, GROUPS, PACK], F32)
+        nc.gpsimd.tensor_scalar(nonneg[:], anc[:], 0.0, None, ALU.is_ge)
+        nc.gpsimd.tensor_scalar(sgn[:], nonneg[:], 2.0, -1.0, ALU.mult, ALU.add)
+
+        v_w = [held("v_w%d" % a, [P, S], U32) for a in range(PASSES)]
+        v_sc = [held("v_sc%d" % a, [P, S], U8) for a in range(PASSES)]
+        for a in range(PASSES):
+            nc.vector.tensor_copy(v_w[a][:], tab_w[a][:].indirect(idx[:]))
+            nc.vector.tensor_copy(v_sc[a][:], tab_sc[:, a * T : (a + 1) * T].indirect(idx[:]))
+
+        w1_bf = {(0, a): held("w1_bf0%d" % a, [P, PACK, P, PACK], BF16)[:] for a in range(PASSES)}
+        w1_w = {(0, a): held("w1_w0%d" % a, [P, KP], U32)[:] for a in range(PASSES)}
+        w1_sc = {(0, a): held("w1_sc0%d" % a, [P, KP], U8)[:] for a in range(PASSES)}
+        w4_dw = {g: held("w4_dw%d" % g, [P, PASSES, PACK, P, 2], U8) for g in range(GROUPS)}
+        w4_dsc = {g: held("w4_dsc%d" % g, [P, PASSES, PACK, P], U8) for g in range(GROUPS)}
+
+        def round_w1(g, a, u, on_vector):
+            dst = w1_bf[g, a][:, :, u * (P // 2) : (u + 1) * (P // 2), :].rearrange("p t m j -> p m t j")
+            src = w1_raw[g, a, u][:].rearrange("p j (m t) -> p m t j", t=PACK)
+            if on_vector:
+                nc.vector.tensor_copy(dst, src)
+            else:
+                nc.scalar.copy(dst, src)
+
+        def quantise_w1(g, a, t0, t1):
+            nc.vector.quantize_mx(
+                out=w1_w[g, a][:, t0 * P : t1 * P].bitcast(E4M3),
+                scales=w1_sc[g, a][:, t0 * P : t1 * P],
+                in_=w1_bf[g, a][:, t0:t1].rearrange("p t m j -> p (t m j)"),
+            )
+
+        def deal_w4(g):
+            nc.vector.tensor_copy(
+                w4_dw[g][:].bitcast(U16).rearrange("p a t m b -> p a m (t b)"),
+                w4_w[g][:].bitcast(U16).rearrange("p (a m t) -> p a m t", a=PASSES, t=PACK),
+            )
+            sc = w4_sc[:].rearrange("p (a c) -> p a c", a=PASSES)[:, :, g * KP : (g + 1) * KP]
+            nc.vector.tensor_copy(
+                w4_dsc[g][:].rearrange("p a t m -> p a m t"), sc.rearrange("p a (m t) -> p a m t", t=PACK)
+            )
+
+        trig = {}
+        lift = {}
+        hval = {}
+        page_pl = {}
+        x_pl = {}
+
+        def first_stage(i):
+            g, t = divmod(i, PACK)
+            cols = slice(t * P, (t + 1) * P)
+            phase = bank(i % 2)
+            lift[i] = bank(2 + i % 6)
+            for a in range(PASSES):
+                nc.tensor.matmul_mx(
+                    phase[:], lhsT=w1_w[g, a][:, cols].bitcast(E4M3), lhsT_scale=w1_sc[g, a][:, cols],
+                    rhs=v_w[a][:].bitcast(E4M3), rhs_scale=v_sc[a][:], start=(a == 0), stop=(a == PASSES - 1),
+                )
+            for a in range(PASSES):
+                nc.tensor.matmul_mx(
+                    lift[i][:], lhsT=w4_dw[g][:, a, t].rearrange("p m b -> p (m b)").bitcast(E2M1),
+                    lhsT_scale=w4_dsc[g][:, a, t, :],
+                    rhs=v_w[a][:].bitcast(E4M3), rhs_scale=v_sc[a][:], start=(a == 0), stop=(a == PASSES - 1),
+                )
+            if i == PACK - 1:
+                dist = held("w1_bf1", [P, S], F32)
+            else:
+                dist = ring.tile([P, S], F32, name="dist")
+            nc.scalar.activation(dist[:], phase[:], ACT.Abs, bias=-math.pi / 4)
+            trig[i] = held("trig%d" % i, [P, S], F32)
+            nc.scalar.activation(trig[i][:], dist[:], ACT.Sin, bias=math.pi / 2, scale=-1.0)
+
+        def product(i):
+            if i == TILES - 1:
+                hval[i] = held("page_bf02", [P, S], F32)
+            elif i == 1:
+                hval[i] = held("w1_w1", [P, S], F32)
+            else:
+                hval[i] = ring.tile([P, S], F32, name="hval")
+            nc.vector.scalar_tensor_tensor(hval[i][:], lift[i][:], root2[:], trig[i][:], ALU.mult, ALU.mult)
+
+        def scatter(i):
+            g, t = divmod(i, PACK)
+            nc.vector.tensor_tensor(page[i][:].indirect(idx2[:]), hval[i][:], wg(t), ALU.mult)
+            nc.scalar.activation(page_pl[g][:, t, :], page[i][:], ACT.Copy, scale=sgn[:, g, t : t + 1])
+
+        def gather(i):
+            g, t = divmod(i, PACK)
+            picked = held("picked%d" % i, [P, PA], F32)
+            nc.vector.tensor_copy(picked[:], page[i][:].indirect(idx3[:]))
+            nc.scalar.activation(x_pl[g][:, t, :], picked[:], ACT.Abs, scale=anc[:, g, t : t + 1])
+
+        page_bf = {(g, c): held("page_bf%d%d" % (g, c), [P, CHUNK, PACK], BF16) for g in range(GROUPS) for c in range(CHUNKS)}
+        page_w = {(g, c): held("page_w%d%d" % (g, c), [P, CHUNK], U32) for g in range(GROUPS) for c in range(CHUNKS)}
+        page_sc = {(g, c): held("page_sc%d%d" % (g, c), [P, CHUNK], U8) for g in range(GROUPS) for c in range(CHUNKS)}
+        x_bf = {g: held("x_bf%d" % g, [P, PA, PACK], BF16) for g in range(GROUPS)}
+        x_w = {g: held("x_w%d" % g, [P, PA], U32) for g in range(GROUPS)}
+        x_sc = {g: held("x_sc%d" % g, [P, PA], U8) for g in range(GROUPS)}
+
+        def weave(dst, planes, on_vector):
+            dst = dst.rearrange("p (c i) t -> p c t i", i=4)
+            planes = planes.rearrange("p t (c i) -> p c t i", i=4)
+            if on_vector:
+                nc.vector.tensor_copy(dst, planes)
+            else:
+                nc.scalar.copy(dst, planes)
+
+        def weave_page(g, c, on_vector):
+            weave(page_bf[g, c][:], page_pl[g][:, :, c * CHUNK : (c + 1) * CHUNK], on_vector)
+
+        def weave_x(g, u, on_vector):
+            cols = slice(u * (PA // 2), (u + 1) * (PA // 2))
+            weave(x_bf[g][:, cols, :], x_pl[g][:, :, cols], on_vector)
+
+        def quantise(words, scales, values):
+            nc.vector.quantize_mx(
+                out=words[:].bitcast(E4M3), scales=scales[:], in_=values[:].rearrange("p c t -> p (c t)")
+            )
+
+        banks = {}
+
+        def second_stage(g, mt):
+            c, w = divmod(mt * P, CHUNK)
+            if g == 0:
+                banks[mt] = bank(mt)
+            nc.tensor.matmul_mx(
+                banks[mt][:], lhsT=page_w[g, c][:, w : w + P].bitcast(E4M3), lhsT_scale=page_sc[g, c][:, w : w + P],
+                rhs=x_w[g][:].bitcast(E4M3), rhs_scale=x_sc[g][:], start=(g == 0), stop=(g == GROUPS - 1),
+            )
+
+        def finish(mt, on_vector):
+            res = held("w1_raw%d%d%d" % (mt // 4, mt // 2 % 2, mt % 2), [P, PA], F32)
+            if on_vector:
+                nc.vector.tensor_scalar(res[:], banks[mt][:], slot_c[:, mt : mt + 1], None, ALU.mult)
+            else:
+                nc.scalar.activation(res[:], banks[mt][:], ACT.Copy, scale=slot_c[:, mt : mt + 1])
+            nc.sync.dma_start(out=out[mt * P : (mt + 1) * P, :], in_=res[:])
+
+        deal_w4(0)
+        round_w1(0, 0, 0, False)
+        round_w1(0, 0, 1, False)
+        round_w1(0, 1, 0, False)
+        quantise_w1(0, 0, 0, PACK)
+        round_w1(0, 1, 1, True)
+        quantise_w1(0, 1, 0, 1)
+        first_stage(0)
+        quantise_w1(0, 1, 1, 2)
+        quantise_w1(0, 1, 2, PACK)
+        deal_w4(1)
+        for i in range(1, PACK):
+            first_stage(i)
+        late_bf = held("w1_bf1", [P, PASSES, PACK, P, PACK], BF16)
+        for a in range(PASSES):
+            w1_bf[1, a] = late_bf[:, a]
+            for u in range(2):
+                round_w1(1, a, u, False)
+        page_pl[0] = held("w1_raw111", [P, PACK, T2], BF16)
+        x_pl[0] = held("w1_raw110", [P, PACK, PA], BF16)
+        page_pl[1] = held("page_pl1", [P, PACK, T2], BF16)
+        x_pl[1] = held("x_pl1", [P, PACK, PA], BF16)
+        product(0)
+
+        for i in range(TILES):
+            if i == TILES - 2:
+                quantise(x_w[0], x_sc[0], x_bf[0])
+                for c in range(CHUNKS - 1):
+                    quantise(page_w[0, c], page_sc[0, c], page_bf[0, c])
+            scatter(i)
+            if i + 1 < TILES:
+                product(i + 1)
+            gather(i)
+            if i == 1:
+                late_w = held("w1_w1", [P, PASSES * KP], U32)
+                late_sc = held("w1_sc1", [P, PASSES * KP], U8)
+                nc.vector.quantize_mx(
+                    out=late_w[:].bitcast(E4M3), scales=late_sc[:],
+                    in_=late_bf[:].rearrange("p a t m j -> p (a t m j)"),
+                )
+                for a in range(PASSES):
+                    w1_w[1, a] = late_w[:, a * KP : (a + 1) * KP]
+                    w1_sc[1, a] = late_sc[:, a * KP : (a + 1) * KP]
+                for n in range(PACK, TILES):
+                    first_stage(n)
+            if i == PACK - 1:
+                weave_x(0, 0, False)
+                weave_x(0, 1, False)
+                for c in range(CHUNKS):
+                    weave_page(0, c, False)
+            if i == TILES - 2:
+                quantise(page_w[0, CHUNKS - 1], page_sc[0, CHUNKS - 1], page_bf[0, CHUNKS - 1])
+                for mt in (0, 1, 4, 5, 6, 7, 2, 3):
+                    second_stage(0, mt)
+
+        weave_page(1, 0, True)
+        weave_page(1, 1, False)
+        weave_x(1, 0, True)
+        weave_x(1, 1, True)
+        weave_page(1, 2, False)
+        quantise(page_w[1, 0], page_sc[1, 0], page_bf[1, 0])
+        quantise(x_w[1], x_sc[1], x_bf[1])
+        quantise(page_w[1, 1], page_sc[1, 1], page_bf[1, 1])
+        weave_page(1, 3, True)
+        quantise(page_w[1, 2], page_sc[1, 2], page_bf[1, 2])
+        quantise(page_w[1, 3], page_sc[1, 3], page_bf[1, 3])
+        for mt in range(T2 // P):
+            second_stage(1, mt)
+            finish(mt, mt % 2 == 1 and mt > 2)

@@ -100,9 +100,12 @@ def tile_list_firework_cue_anchors_kernel(
             nc.sync.dma_start(
                 out=tab_w[a][:].bitcast(I32), in_=tab_words[a].rearrange("p n t -> p (n t)").bitcast(I32)
             )
+            if a == 0:
+                load_scales(nc.sync, tab_sc, tab_scales)
+        anc = held("anc", [P, GROUPS, PACK], F32)
+        nc.gpsimd.dma_start(out=anc[:], in_=anchor.rearrange("(g p t) -> p g t", g=GROUPS, t=PACK))
         load_w4(0)
-        load_scales(nc.scalar, tab_sc, tab_scales)
-        load_scales(nc.gpsimd, w4_sc, w4_scales)
+        load_scales(nc.sync, w4_sc, w4_scales)
         for a in range(PASSES):
             for u in range(2):
                 load_w1(0, a, u)
@@ -114,8 +117,6 @@ def tile_list_firework_cue_anchors_kernel(
         nc.sync.dma_start(out=idx3[:], in_=offs3)
         for q in range(4):
             nc.sync.dma_start(out=wg_rest[32 * q : 32 * (q + 1)], in_=wgs_rows[:, 1:PACK, :])
-        anc = held("anc", [P, GROUPS, PACK], F32)
-        nc.sync.dma_start(out=anc[:], in_=anchor.rearrange("(g p t) -> p g t", g=GROUPS, t=PACK))
         load_page(1)
         for a in range(PASSES):
             for u in range(2):
@@ -131,17 +132,18 @@ def tile_list_firework_cue_anchors_kernel(
         nc.gpsimd.tensor_scalar(nonneg[:], anc[:], 0.0, None, ALU.is_ge)
         nc.gpsimd.tensor_scalar(sgn[:], nonneg[:], 2.0, -1.0, ALU.mult, ALU.add)
 
-        v_w = [held("v_w%d" % a, [P, S], U32) for a in range(PASSES)]
+        v_w = [held("v_w0", [P, S], U32)]
         v_sc = [held("v_sc%d" % a, [P, S], U8) for a in range(PASSES)]
+        nc.vector.tensor_copy(v_w[0][:], tab_w[0][:].indirect(idx[:]))
         for a in range(PASSES):
-            nc.vector.tensor_copy(v_w[a][:], tab_w[a][:].indirect(idx[:]))
             nc.vector.tensor_copy(v_sc[a][:], tab_sc[:, a * T : (a + 1) * T].indirect(idx[:]))
+        v_w.append(held("tab_sc", [P, S], U32))
+        nc.vector.tensor_copy(v_w[1][:], tab_w[1][:].indirect(idx[:]))
 
-        w1_bf = {(0, a): held("w1_bf0%d" % a, [P, PACK, P, PACK], BF16)[:] for a in range(PASSES)}
-        w1_w = {(0, a): held("w1_w0%d" % a, [P, KP], U32)[:] for a in range(PASSES)}
+        w1_bf = {(0, 0): held("w1_bf00", [P, PACK, P, PACK], BF16)[:]}
+        w1_w = {(0, 1): held("w1_w01", [P, KP], U32)[:]}
         w1_sc = {(0, a): held("w1_sc0%d" % a, [P, KP], U8)[:] for a in range(PASSES)}
-        w4_dw = {g: held("w4_dw%d" % g, [P, PASSES, PACK, P, 2], U8) for g in range(GROUPS)}
-        w4_dsc = {g: held("w4_dsc%d" % g, [P, PASSES, PACK, P], U8) for g in range(GROUPS)}
+        w4_dw = {}
 
         def round_w1(g, a, u, on_vector):
             dst = w1_bf[g, a][:, :, u * (P // 2) : (u + 1) * (P // 2), :].rearrange("p t m j -> p m t j")
@@ -159,14 +161,18 @@ def tile_list_firework_cue_anchors_kernel(
             )
 
         def deal_w4(g):
+            w4_dw[g] = held(("tab_w1", "w1_bf00")[g], [P, PASSES, PACK, P, 2], U8)
             nc.vector.tensor_copy(
                 w4_dw[g][:].bitcast(U16).rearrange("p a t m b -> p a m (t b)"),
                 w4_w[g][:].bitcast(U16).rearrange("p (a m t) -> p a m t", a=PASSES, t=PACK),
             )
-            sc = w4_sc[:].rearrange("p (a c) -> p a c", a=PASSES)[:, :, g * KP : (g + 1) * KP]
+
+        def deal_w4_scales():
+            dealt = held("w4_w0", [P, PASSES * GROUPS, PACK, P], U8)
             nc.vector.tensor_copy(
-                w4_dsc[g][:].rearrange("p a t m -> p a m t"), sc.rearrange("p a (m t) -> p a m t", t=PACK)
+                dealt[:].rearrange("p n t m -> p n m t"), w4_sc[:].rearrange("p (n m t) -> p n m t", m=P, t=PACK)
             )
+            return dealt
 
         trig = {}
         lift = {}
@@ -177,17 +183,18 @@ def tile_list_firework_cue_anchors_kernel(
         def first_stage(i):
             g, t = divmod(i, PACK)
             cols = slice(t * P, (t + 1) * P)
-            phase = bank(i % 2)
-            lift[i] = bank(2 + i % 6)
-            for a in range(PASSES):
+            phase = bank((0, 1, 2, 3, 5, 6, 7, 3)[i])
+            order = (0, 1) if i == 0 else (1, 0)
+            for a in order:
                 nc.tensor.matmul_mx(
                     phase[:], lhsT=w1_w[g, a][:, cols].bitcast(E4M3), lhsT_scale=w1_sc[g, a][:, cols],
-                    rhs=v_w[a][:].bitcast(E4M3), rhs_scale=v_sc[a][:], start=(a == 0), stop=(a == PASSES - 1),
+                    rhs=v_w[a][:].bitcast(E4M3), rhs_scale=v_sc[a][:], start=(a == order[0]), stop=(a == order[1]),
                 )
+            lift[i] = bank((4, 0, 1, 2, 4, 5, 6, 7)[i])
             for a in range(PASSES):
                 nc.tensor.matmul_mx(
                     lift[i][:], lhsT=w4_dw[g][:, a, t].rearrange("p m b -> p (m b)").bitcast(E2M1),
-                    lhsT_scale=w4_dsc[g][:, a, t, :],
+                    lhsT_scale=w4_dsc[:, a * GROUPS + g, t, :],
                     rhs=v_w[a][:].bitcast(E4M3), rhs_scale=v_sc[a][:], start=(a == 0), stop=(a == PASSES - 1),
                 )
             if i == PACK - 1:
@@ -201,22 +208,23 @@ def tile_list_firework_cue_anchors_kernel(
         def product(i):
             if i == TILES - 1:
                 hval[i] = held("page_bf02", [P, S], F32)
-            elif i == 1:
-                hval[i] = held("w1_w1", [P, S], F32)
             else:
-                hval[i] = ring.tile([P, S], F32, name="hval")
+                hval[i] = held("hval", [P, S], F32)
             nc.vector.scalar_tensor_tensor(hval[i][:], lift[i][:], root2[:], trig[i][:], ALU.mult, ALU.mult)
 
         def scatter(i):
             g, t = divmod(i, PACK)
             nc.vector.tensor_tensor(page[i][:].indirect(idx2[:]), hval[i][:], wg(t), ALU.mult)
-            nc.scalar.activation(page_pl[g][:, t, :], page[i][:], ACT.Copy, scale=sgn[:, g, t : t + 1])
 
-        def gather(i):
+        def round_page(i, c0, c1):
             g, t = divmod(i, PACK)
-            picked = held("picked%d" % i, [P, PA], F32)
-            nc.vector.tensor_copy(picked[:], page[i][:].indirect(idx3[:]))
-            nc.scalar.activation(x_pl[g][:, t, :], picked[:], ACT.Abs, scale=anc[:, g, t : t + 1])
+            nc.scalar.activation(page_pl[g][:, t, c0:c1], page[i][:, c0:c1], ACT.Copy, scale=sgn[:, g, t : t + 1])
+
+        def gather(i, j0, j1):
+            g, t = divmod(i, PACK)
+            picked = held("picked%d_%d" % (i, j0), [P, j1 - j0], F32)
+            nc.vector.tensor_copy(picked[:], page[i][:].indirect(idx3[:, j0 // 16 : j1 // 16]))
+            nc.scalar.activation(x_pl[g][:, t, j0:j1], picked[:], ACT.Abs, scale=anc[:, g, t : t + 1])
 
         page_bf = {(g, c): held("page_bf%d%d" % (g, c), [P, CHUNK, PACK], BF16) for g in range(GROUPS) for c in range(CHUNKS)}
         page_w = {(g, c): held("page_w%d%d" % (g, c), [P, CHUNK], U32) for g in range(GROUPS) for c in range(CHUNKS)}
@@ -265,10 +273,13 @@ def tile_list_firework_cue_anchors_kernel(
             nc.sync.dma_start(out=out[mt * P : (mt + 1) * P, :], in_=res[:])
 
         deal_w4(0)
+        w4_dsc = deal_w4_scales()
+        w1_w[0, 0] = held("w4_sc", [P, KP], U32)[:]
         round_w1(0, 0, 0, False)
         round_w1(0, 0, 1, False)
-        round_w1(0, 1, 0, False)
         quantise_w1(0, 0, 0, PACK)
+        w1_bf[0, 1] = held("w1_bf00", [P, PACK, P, PACK], BF16)[:]
+        round_w1(0, 1, 0, False)
         round_w1(0, 1, 1, True)
         quantise_w1(0, 1, 0, 1)
         first_stage(0)
@@ -294,11 +305,13 @@ def tile_list_firework_cue_anchors_kernel(
                 for c in range(CHUNKS - 1):
                     quantise(page_w[0, c], page_sc[0, c], page_bf[0, c])
             scatter(i)
-            if i + 1 < TILES:
-                product(i + 1)
-            gather(i)
+            if i + 1 == TILES:
+                break
+            round_page(i, 0, T2)
+            product(i + 1)
+            gather(i, 0, PA)
             if i == 1:
-                late_w = held("w1_w1", [P, PASSES * KP], U32)
+                late_w = held("trig2", [P, PASSES * KP], U32)
                 late_sc = held("w1_sc1", [P, PASSES * KP], U8)
                 nc.vector.quantize_mx(
                     out=late_w[:].bitcast(E4M3), scales=late_sc[:],
@@ -316,20 +329,24 @@ def tile_list_firework_cue_anchors_kernel(
                     weave_page(0, c, False)
             if i == TILES - 2:
                 quantise(page_w[0, CHUNKS - 1], page_sc[0, CHUNKS - 1], page_bf[0, CHUNKS - 1])
-                for mt in (0, 1, 4, 5, 6, 7, 2, 3):
+                for mt in range(T2 // P):
                     second_stage(0, mt)
 
+        last = TILES - 1
+        round_page(last, 0, CHUNK)
+        gather(last, 0, PA // 2)
+        gather(last, PA // 2, PA)
+        round_page(last, CHUNK, T2)
         weave_page(1, 0, True)
-        weave_page(1, 1, False)
         weave_x(1, 0, True)
         weave_x(1, 1, True)
+        weave_page(1, 1, False)
         weave_page(1, 2, False)
         quantise(page_w[1, 0], page_sc[1, 0], page_bf[1, 0])
         quantise(x_w[1], x_sc[1], x_bf[1])
-        quantise(page_w[1, 1], page_sc[1, 1], page_bf[1, 1])
         weave_page(1, 3, True)
-        quantise(page_w[1, 2], page_sc[1, 2], page_bf[1, 2])
-        quantise(page_w[1, 3], page_sc[1, 3], page_bf[1, 3])
+        for c in range(1, CHUNKS):
+            quantise(page_w[1, c], page_sc[1, c], page_bf[1, c])
         for mt in range(T2 // P):
             second_stage(1, mt)
             finish(mt, mt % 2 == 1 and mt > 2)

@@ -82,10 +82,10 @@ def tile_list_firework_cue_anchors_kernel(
             nc.sync.dma_start(out=page[i][:], in_=rows[:, t, :])
 
         def load_scales(queue, dst, src):
-            for q in range(4):
+            for r in range(4):
                 queue.dma_start(
-                    out=dst[32 * q : 32 * q + 4, :].bitcast(I32).rearrange("r (a n) -> r a n", a=PASSES),
-                    in_=src[:, 4 * q : 4 * q + 4, :].bitcast(I32).rearrange("a r n -> r a n"),
+                    out=dst[r:P:32, :].bitcast(I32).rearrange("q (a n) -> q a n", a=PASSES),
+                    in_=src[:, r:16:4, :].bitcast(I32).rearrange("a q n -> q a n"),
                 )
 
         wgs_rows = wgs.rearrange("(q t) j -> q t j", t=PACK)
@@ -110,12 +110,12 @@ def tile_list_firework_cue_anchors_kernel(
             for u in range(2):
                 load_w1(0, a, u)
         load_w4(1)
-        for q in range(4):
+        for q in (0, 2, 1, 3):
             nc.sync.dma_start(out=wg_first[32 * q : 32 * (q + 1)], in_=wgs_rows[:, 0:1, :])
         nc.sync.dma_start(out=idx2[:], in_=offs2)
         load_page(0)
         nc.sync.dma_start(out=idx3[:], in_=offs3)
-        for q in range(4):
+        for q in (0, 2, 1, 3):
             nc.sync.dma_start(out=wg_rest[32 * q : 32 * (q + 1)], in_=wgs_rows[:, 1:PACK, :])
         load_page(1)
         for a in range(PASSES):
@@ -163,14 +163,14 @@ def tile_list_firework_cue_anchors_kernel(
         def deal_w4(g):
             w4_dw[g] = held(("tab_w1", "w1_bf00")[g], [P, PASSES, PACK, P, 2], U8)
             nc.vector.tensor_copy(
-                w4_dw[g][:].bitcast(U16).rearrange("p a t m b -> p a m (t b)"),
-                w4_w[g][:].bitcast(U16).rearrange("p (a m t) -> p a m t", a=PASSES, t=PACK),
+                w4_dw[g][:].bitcast(U16).rearrange("p a t m b -> p a t (m b)"),
+                w4_w[g][:].bitcast(U16).rearrange("p (a m t) -> p a t m", a=PASSES, t=PACK),
             )
 
         def deal_w4_scales():
             dealt = held("w4_w0", [P, PASSES * GROUPS, PACK, P], U8)
             nc.vector.tensor_copy(
-                dealt[:].rearrange("p n t m -> p n m t"), w4_sc[:].rearrange("p (n m t) -> p n m t", m=P, t=PACK)
+                dealt[:], w4_sc[:].rearrange("p (n m t) -> p n t m", m=P, t=PACK)
             )
             return dealt
 
@@ -209,7 +209,7 @@ def tile_list_firework_cue_anchors_kernel(
             if i == TILES - 1:
                 hval[i] = held("page_bf02", [P, S], F32)
             else:
-                hval[i] = held("hval", [P, S], F32)
+                hval[i] = ring.tile([P, S], F32, name="hval")
             nc.vector.scalar_tensor_tensor(hval[i][:], lift[i][:], root2[:], trig[i][:], ALU.mult, ALU.mult)
 
         def scatter(i):
@@ -229,29 +229,29 @@ def tile_list_firework_cue_anchors_kernel(
         page_bf = {(g, c): held("page_bf%d%d" % (g, c), [P, CHUNK, PACK], BF16) for g in range(GROUPS) for c in range(CHUNKS)}
         page_w = {(g, c): held("page_w%d%d" % (g, c), [P, CHUNK], U32) for g in range(GROUPS) for c in range(CHUNKS)}
         page_sc = {(g, c): held("page_sc%d%d" % (g, c), [P, CHUNK], U8) for g in range(GROUPS) for c in range(CHUNKS)}
-        x_bf = {g: held("x_bf%d" % g, [P, PA, PACK], BF16) for g in range(GROUPS)}
+        x_bf = {(g, u): held("x_bf%d%d" % (g, u), [P, PA // 2, PACK], BF16) for g in range(GROUPS) for u in range(2)}
         x_w = {g: held("x_w%d" % g, [P, PA], U32) for g in range(GROUPS)}
         x_sc = {g: held("x_sc%d" % g, [P, PA], U8) for g in range(GROUPS)}
 
-        def weave(dst, planes, on_vector):
-            dst = dst.rearrange("p (c i) t -> p c t i", i=4)
-            planes = planes.rearrange("p t (c i) -> p c t i", i=4)
-            if on_vector:
-                nc.vector.tensor_copy(dst, planes)
-            else:
-                nc.scalar.copy(dst, planes)
+        def weave(dst, planes):
+            dst = dst[:, :, 0 : planes.shape[1]].rearrange("p (c i) t -> p c t i", i=4)
+            nc.scalar.copy(dst, planes.rearrange("p t (c i) -> p c t i", i=4))
 
-        def weave_page(g, c, on_vector):
-            weave(page_bf[g, c][:], page_pl[g][:, :, c * CHUNK : (c + 1) * CHUNK], on_vector)
-
-        def weave_x(g, u, on_vector):
-            cols = slice(u * (PA // 2), (u + 1) * (PA // 2))
-            weave(x_bf[g][:, cols, :], x_pl[g][:, :, cols], on_vector)
+        def weave_group(g):
+            for u in range(2):
+                weave(x_bf[g, u], x_pl[g][:, :, u * CHUNK : (u + 1) * CHUNK])
+            for c in range(CHUNKS):
+                weave(page_bf[g, c], page_pl[g][:, :, c * CHUNK : (c + 1) * CHUNK])
 
         def quantise(words, scales, values):
-            nc.vector.quantize_mx(
-                out=words[:].bitcast(E4M3), scales=scales[:], in_=values[:].rearrange("p c t -> p (c t)")
-            )
+            nc.vector.quantize_mx(out=words.bitcast(E4M3), scales=scales, in_=values[:].rearrange("p c t -> p (c t)"))
+
+        def quantise_page(g, c):
+            quantise(page_w[g, c][:], page_sc[g, c][:], page_bf[g, c])
+
+        def quantise_x(g, u):
+            cols = slice(u * CHUNK, (u + 1) * CHUNK)
+            quantise(x_w[g][:, cols], x_sc[g][:, cols], x_bf[g, u])
 
         banks = {}
 
@@ -295,15 +295,16 @@ def tile_list_firework_cue_anchors_kernel(
                 round_w1(1, a, u, False)
         page_pl[0] = held("w1_raw111", [P, PACK, T2], BF16)
         x_pl[0] = held("w1_raw110", [P, PACK, PA], BF16)
-        page_pl[1] = held("page_pl1", [P, PACK, T2], BF16)
-        x_pl[1] = held("x_pl1", [P, PACK, PA], BF16)
+        page_pl[1] = held("page_pl1", [P, PACK - 1, T2], BF16)
+        x_pl[1] = held("x_pl1", [P, PACK - 1, PA], BF16)
         product(0)
 
         for i in range(TILES):
             if i == TILES - 2:
-                quantise(x_w[0], x_sc[0], x_bf[0])
+                for u in range(2):
+                    quantise_x(0, u)
                 for c in range(CHUNKS - 1):
-                    quantise(page_w[0, c], page_sc[0, c], page_bf[0, c])
+                    quantise_page(0, c)
             scatter(i)
             if i + 1 == TILES:
                 break
@@ -323,30 +324,41 @@ def tile_list_firework_cue_anchors_kernel(
                 for n in range(PACK, TILES):
                     first_stage(n)
             if i == PACK - 1:
-                weave_x(0, 0, False)
-                weave_x(0, 1, False)
-                for c in range(CHUNKS):
-                    weave_page(0, c, False)
+                weave_group(0)
             if i == TILES - 2:
-                quantise(page_w[0, CHUNKS - 1], page_sc[0, CHUNKS - 1], page_bf[0, CHUNKS - 1])
+                weave_group(1)
+                quantise_page(0, CHUNKS - 1)
                 for mt in range(T2 // P):
                     second_stage(0, mt)
 
         last = TILES - 1
-        round_page(last, 0, CHUNK)
-        gather(last, 0, PA // 2)
-        gather(last, PA // 2, PA)
-        round_page(last, CHUNK, T2)
-        weave_page(1, 0, True)
-        weave_x(1, 0, True)
-        weave_x(1, 1, True)
-        weave_page(1, 1, False)
-        weave_page(1, 2, False)
-        quantise(page_w[1, 0], page_sc[1, 0], page_bf[1, 0])
-        quantise(x_w[1], x_sc[1], x_bf[1])
-        weave_page(1, 3, True)
-        for c in range(1, CHUNKS):
-            quantise(page_w[1, c], page_sc[1, c], page_bf[1, c])
+        last_sign = held("page_pl1", [P, 1], F32)
+        nc.scalar.copy(last_sign[:], sgn[:, GROUPS - 1, PACK - 1 : PACK])
+
+        def last_x(u):
+            picked = held("picked_last%d" % u, [P, CHUNK], F32)
+            nc.vector.tensor_copy(picked[:], page[last][:].indirect(idx3[:, u * CHUNK // 16 : (u + 1) * CHUNK // 16]))
+            nc.scalar.activation(
+                x_bf[1, u][:, :, PACK - 1], picked[:], ACT.Abs, scale=anc[:, GROUPS - 1, PACK - 1 : PACK]
+            )
+
+        def last_page(c):
+            nc.vector.tensor_scalar(
+                page_bf[1, c][:, :, PACK - 1], page[last][:, c * CHUNK : (c + 1) * CHUNK], last_sign[:], None, ALU.mult
+            )
+
+        last_x(0)
+        last_x(1)
+        last_page(0)
+        last_page(1)
+        quantise_page(1, 0)
+        quantise_x(1, 0)
+        quantise_x(1, 1)
+        last_page(2)
+        quantise_page(1, 1)
+        last_page(3)
+        quantise_page(1, 2)
+        quantise_page(1, 3)
         for mt in range(T2 // P):
             second_stage(1, mt)
-            finish(mt, mt % 2 == 1 and mt > 2)
+            finish(mt, mt in (5, 7))

import math
from contextlib import ExitStack

import concourse.mybir as mybir

K, H, T, S, T2, PA = 1024, 1024, 2048, 512, 1024, 512
FLOPS = 2 * (2 * K * H * S + H * T2 * PA)

F32 = mybir.dt.float32
BF16 = mybir.dt.bfloat16
I32 = mybir.dt.int32
U32 = mybir.dt.uint32
U16 = mybir.dt.uint16
U8 = mybir.dt.uint8
E4M3 = mybir.dt.float8_e4m3fn_x4
E2M1 = mybir.dt.float4_e2m1fn_x4
ALU = mybir.AluOpType
ACT = mybir.ActivationFunctionType

P = 128
PACK = 4
KP = P * PACK
PASSES = K // KP
GROUPS = H // KP
TILES = GROUPS * PACK
HALF = KP // 2
CHUNK = 256
CHUNKS = T2 // CHUNK


def tile_list_firework_cue_anchors_kernel(
    tc, tab_words, tab_scales, w1, w4_words, w4_scales, wgs, page0, anchor, slot, offs, offs2, offs3, out
):
    nc = tc.nc
    with ExitStack() as ctx:
        lists = ctx.enter_context(tc.tile_pool(name="lists", bufs=1))
        keep = ctx.enter_context(tc.tile_pool(name="keep", bufs=1))
        ring = ctx.enter_context(tc.tile_pool(name="ring", bufs=2))
        psum = ctx.enter_context(tc.psum_pool(name="psum", bufs=1))

        def held(name, shape, dtype):
            return keep.tile(shape, dtype, name=name, align_bytes=64)

        def bank(b):
            return psum.tile([P, KP], F32, name="bank%d" % b)

        tab_sc = held("tab_sc", [P, PASSES * T], U8)
        w4_sc = held("w4_sc", [P, PASSES * H], U8)
        zero = held("zero", [P, 1], F32)
        nc.vector.memset(tab_sc[:].bitcast(I32), 0)
        nc.vector.memset(w4_sc[:].bitcast(I32), 0)
        nc.vector.memset(zero[:], 0.0)
        sin45 = held("sin45", [P, 1], F32)
        root2 = held("root2", [P, 1], F32)
        nc.scalar.activation(sin45[:], zero[:], ACT.Sin, bias=math.pi / 4)
        nc.vector.reciprocal(root2[:], sin45[:])

        idx = lists.tile([P, S // 16], U16, name="idx")
        idx2 = lists.tile([P, S // 16], U16, name="idx2")
        idx3 = lists.tile([P, PA // 16], U16, name="idx3")
        tab_w = [held("tab_w%d" % a, [P, T], U32) for a in range(PASSES)]
        w1_raw = {}
        w4_w = {}
        page = {}

        def load_w1(g, a, u):
            w1_raw[g, a, u] = held("w1_raw%d%d%d" % (g, a, u), [P, PACK, HALF], F32)
            rows = w1[a * KP : (a + 1) * KP, g * KP + u * HALF : g * KP + (u + 1) * HALF]
            nc.sync.dma_start(out=w1_raw[g, a, u][:], in_=rows.rearrange("(p j) c -> p j c", j=PACK))

        def load_w4(g):
            w4_w[g] = held("w4_w%d" % g, [P, PASSES * 2 * KP], U8)
            nc.sync.dma_start(
                out=w4_w[g][:].bitcast(I32).rearrange("p (a n) -> p a n", a=PASSES),
                in_=w4_words[:, :, 2 * KP * g : 2 * KP * (g + 1)].bitcast(I32).rearrange("a p n -> p a n"),
            )

        def load_page(i):
            g, t = divmod(i, PACK)
            page[i] = held("page%d" % i, [P, T2], F32)
            rows = page0[g * KP : (g + 1) * KP, :].rearrange("(p t) m -> p t m", t=PACK)
            nc.sync.dma_start(out=page[i][:], in_=rows[:, t, :])

        def load_scales(queue, dst, src):
            for r in range(4):
                queue.dma_start(
                    out=dst[r:P:32, :].bitcast(I32).rearrange("q (a n) -> q a n", a=PASSES),
                    in_=src[:, r:16:4, :].bitcast(I32).rearrange("a q n -> q a n"),
                )

        wgs_rows = wgs.rearrange("(q t) j -> q t j", t=PACK)
        wg_first = held("wg_first", [P, 1, S], F32)
        wg_rest = held("wg_rest", [P, PACK - 1, S], F32)

        def wg(t):
            return wg_first[:, 0, :] if t == 0 else wg_rest[:, t - 1, :]

        nc.sync.dma_start(out=idx[:], in_=offs)
        for a in range(PASSES):
            nc.sync.dma_start(
                out=tab_w[a][:].bitcast(I32), in_=tab_words[a].rearrange("p n t -> p (n t)").bitcast(I32)
            )
            if a == 0:
                load_scales(nc.sync, tab_sc, tab_scales)
        anc = held("anc", [P, GROUPS, PACK], F32)
        nc.gpsimd.dma_start(out=anc[:], in_=anchor.rearrange("(g p t) -> p g t", g=GROUPS, t=PACK))
        load_w4(0)
        load_scales(nc.sync, w4_sc, w4_scales)
        for a in range(PASSES):
            for u in range(2):
                load_w1(0, a, u)
        load_w4(1)
        for q in (0, 2, 1, 3):
            nc.sync.dma_start(out=wg_first[32 * q : 32 * (q + 1)], in_=wgs_rows[:, 0:1, :])
        nc.sync.dma_start(out=idx2[:], in_=offs2)
        load_page(0)
        nc.sync.dma_start(out=idx3[:], in_=offs3)
        for q in (0, 2, 1, 3):
            nc.sync.dma_start(out=wg_rest[32 * q : 32 * (q + 1)], in_=wgs_rows[:, 1:PACK, :])
        load_page(1)
        for a in range(PASSES):
            for u in range(2):
                load_w1(1, a, u)
        for i in range(2, TILES):
            load_page(i)

        slot_c = held("slot_c", [P, T2 // P], F32)
        with nc.allow_non_contiguous_dma(reason="one factor a partition"):
            nc.sync.dma_start(out=slot_c[:], in_=slot.rearrange("(c p) -> p c", p=P))
        nonneg = held("nonneg", [P, GROUPS, PACK], F32)
        sgn = held("sgn", [P, GROUPS, PACK], F32)
        nc.gpsimd.tensor_scalar(nonneg[:], anc[:], 0.0, None, ALU.is_ge)
        nc.gpsimd.tensor_scalar(sgn[:], nonneg[:], 2.0, -1.0, ALU.mult, ALU.add)

        v_w = [held("v_w0", [P, S], U32)]
        v_sc = [held("v_sc%d" % a, [P, S], U8) for a in range(PASSES)]
        nc.vector.tensor_copy(v_w[0][:], tab_w[0][:].indirect(idx[:]))
        for a in range(PASSES):
            nc.vector.tensor_copy(v_sc[a][:], tab_sc[:, a * T : (a + 1) * T].indirect(idx[:]))
        v_w.append(held("tab_sc", [P, S], U32))
        nc.vector.tensor_copy(v_w[1][:], tab_w[1][:].indirect(idx[:]))

        w1_bf = {(0, 0): held("w1_bf00", [P, PACK, P, PACK], BF16)[:]}
        w1_w = {(0, 1): held("w1_w01", [P, KP], U32)[:]}
        w1_sc = {(0, a): held("w1_sc0%d" % a, [P, KP], U8)[:] for a in range(PASSES)}
        w4_dw = {}

        def round_w1(g, a, u, on_vector):
            dst = w1_bf[g, a][:, :, u * (P // 2) : (u + 1) * (P // 2), :].rearrange("p t m j -> p m t j")
            src = w1_raw[g, a, u][:].rearrange("p j (m t) -> p m t j", t=PACK)
            if on_vector:
                nc.vector.tensor_copy(dst, src)
            else:
                nc.scalar.copy(dst, src)

        def quantise_w1(g, a, t0, t1):
            nc.vector.quantize_mx(
                out=w1_w[g, a][:, t0 * P : t1 * P].bitcast(E4M3),
                scales=w1_sc[g, a][:, t0 * P : t1 * P],
                in_=w1_bf[g, a][:, t0:t1].rearrange("p t m j -> p (t m j)"),
            )

        def deal_w4(g):
            w4_dw[g] = held(("tab_w1", "w1_bf00")[g], [P, PASSES, PACK, P, 2], U8)
            nc.vector.tensor_copy(
                w4_dw[g][:].bitcast(U16).rearrange("p a t m b -> p a t (m b)"),
                w4_w[g][:].bitcast(U16).rearrange("p (a m t) -> p a t m", a=PASSES, t=PACK),
            )

        def deal_w4_scales():
            dealt = held("w4_w0", [P, PASSES * GROUPS, PACK, P], U8)
            nc.vector.tensor_copy(
                dealt[:], w4_sc[:].rearrange("p (n m t) -> p n t m", m=P, t=PACK)
            )
            return dealt

        trig = {}
        lift = {}
        hval = {}
        page_pl = {}
        x_pl = {}

        def first_stage(i):
            g, t = divmod(i, PACK)
            cols = slice(t * P, (t + 1) * P)
            phase = bank((0, 1, 2, 3, 5, 6, 7, 3)[i])
            order = (0, 1) if i == 0 else (1, 0)
            for a in order:
                nc.tensor.matmul_mx(
                    phase[:], lhsT=w1_w[g, a][:, cols].bitcast(E4M3), lhsT_scale=w1_sc[g, a][:, cols],
                    rhs=v_w[a][:].bitcast(E4M3), rhs_scale=v_sc[a][:], start=(a == order[0]), stop=(a == order[1]),
                )
            lift[i] = bank((4, 0, 1, 2, 4, 5, 6, 7)[i])
            for a in range(PASSES):
                nc.tensor.matmul_mx(
                    lift[i][:], lhsT=w4_dw[g][:, a, t].rearrange("p m b -> p (m b)").bitcast(E2M1),
                    lhsT_scale=w4_dsc[:, a * GROUPS + g, t, :],
                    rhs=v_w[a][:].bitcast(E4M3), rhs_scale=v_sc[a][:], start=(a == 0), stop=(a == PASSES - 1),
                )
            if i == PACK - 1:
                dist = held("w1_bf1", [P, S], F32)
            else:
                dist = ring.tile([P, S], F32, name="dist")
            nc.scalar.activation(dist[:], phase[:], ACT.Abs, bias=-math.pi / 4)
            trig[i] = held("trig%d" % i, [P, S], F32)
            nc.scalar.activation(trig[i][:], dist[:], ACT.Sin, bias=math.pi / 2, scale=-1.0)

        def product(i):
            if i == TILES - 1:
                hval[i] = held("page_bf02", [P, S], F32)
            else:
                hval[i] = ring.tile([P, S], F32, name="hval")
            nc.vector.scalar_tensor_tensor(hval[i][:], lift[i][:], root2[:], trig[i][:], ALU.mult, ALU.mult)

        def scatter(i):
            g, t = divmod(i, PACK)
            nc.vector.tensor_tensor(page[i][:].indirect(idx2[:]), hval[i][:], wg(t), ALU.mult)

        def round_page(i, c0, c1):
            g, t = divmod(i, PACK)
            nc.scalar.activation(page_pl[g][:, t, c0:c1], page[i][:, c0:c1], ACT.Copy, scale=sgn[:, g, t : t + 1])

        def gather(i, j0, j1):
            g, t = divmod(i, PACK)
            picked = held("picked%d_%d" % (i, j0), [P, j1 - j0], F32)
            nc.vector.tensor_copy(picked[:], page[i][:].indirect(idx3[:, j0 // 16 : j1 // 16]))
            nc.scalar.activation(x_pl[g][:, t, j0:j1], picked[:], ACT.Abs, scale=anc[:, g, t : t + 1])

        page_bf = {(g, c): held("page_bf%d%d" % (g, c), [P, CHUNK, PACK], BF16) for g in range(GROUPS) for c in range(CHUNKS)}
        page_w = {(g, c): held("page_w%d%d" % (g, c), [P, CHUNK], U32) for g in range(GROUPS) for c in range(CHUNKS)}
        page_sc = {(g, c): held("page_sc%d%d" % (g, c), [P, CHUNK], U8) for g in range(GROUPS) for c in range(CHUNKS)}
        x_bf = {(g, u): held("x_bf%d%d" % (g, u), [P, PA // 2, PACK], BF16) for g in range(GROUPS) for u in range(2)}
        x_w = {g: held("x_w%d" % g, [P, PA], U32) for g in range(GROUPS)}
        x_sc = {g: held("x_sc%d" % g, [P, PA], U8) for g in range(GROUPS)}

        def weave(dst, planes):
            dst = dst[:, :, 0 : planes.shape[1]].rearrange("p (c i) t -> p c t i", i=4)
            nc.scalar.copy(dst, planes.rearrange("p t (c i) -> p c t i", i=4))

        def weave_group(g):
            for u in range(2):
                weave(x_bf[g, u], x_pl[g][:, :, u * CHUNK : (u + 1) * CHUNK])
            for c in range(CHUNKS):
                weave(page_bf[g, c], page_pl[g][:, :, c * CHUNK : (c + 1) * CHUNK])

        def quantise(words, scales, values):
            nc.vector.quantize_mx(out=words.bitcast(E4M3), scales=scales, in_=values[:].rearrange("p c t -> p (c t)"))

        def quantise_page(g, c):
            quantise(page_w[g, c][:], page_sc[g, c][:], page_bf[g, c])

        def quantise_x(g, u):
            cols = slice(u * CHUNK, (u + 1) * CHUNK)
            quantise(x_w[g][:, cols], x_sc[g][:, cols], x_bf[g, u])

        banks = {}

        def second_stage(g, mt):
            c, w = divmod(mt * P, CHUNK)
            if g == 0:
                banks[mt] = bank(mt)
            nc.tensor.matmul_mx(
                banks[mt][:], lhsT=page_w[g, c][:, w : w + P].bitcast(E4M3), lhsT_scale=page_sc[g, c][:, w : w + P],
                rhs=x_w[g][:].bitcast(E4M3), rhs_scale=x_sc[g][:], start=(g == 0), stop=(g == GROUPS - 1),
            )

        def finish(mt, on_vector):
            res = held("w1_raw%d%d%d" % (mt // 4, mt // 2 % 2, mt % 2), [P, PA], F32)
            if on_vector:
                nc.vector.tensor_scalar(res[:], banks[mt][:], slot_c[:, mt : mt + 1], None, ALU.mult)
            else:
                nc.scalar.activation(res[:], banks[mt][:], ACT.Copy, scale=slot_c[:, mt : mt + 1])
            nc.sync.dma_start(out=out[mt * P : (mt + 1) * P, :], in_=res[:])

        deal_w4(0)
        w4_dsc = deal_w4_scales()
        w1_w[0, 0] = held("w4_sc", [P, KP], U32)[:]
        round_w1(0, 0, 0, False)
        round_w1(0, 0, 1, False)
        quantise_w1(0, 0, 0, PACK)
        w1_bf[0, 1] = held("w1_bf00", [P, PACK, P, PACK], BF16)[:]
        round_w1(0, 1, 0, False)
        round_w1(0, 1, 1, True)
        quantise_w1(0, 1, 0, 1)
        first_stage(0)
        quantise_w1(0, 1, 1, 2)
        quantise_w1(0, 1, 2, PACK)
        deal_w4(1)
        for i in range(1, PACK):
            first_stage(i)
        late_bf = held("w1_bf1", [P, PASSES, PACK, P, PACK], BF16)
        for a in range(PASSES):
            w1_bf[1, a] = late_bf[:, a]
            for u in range(2):
                round_w1(1, a, u, False)
        page_pl[0] = held("w1_raw111", [P, PACK, T2], BF16)
        x_pl[0] = held("w1_raw110", [P, PACK, PA], BF16)
        page_pl[1] = held("page_pl1", [P, PACK - 1, T2], BF16)
        x_pl[1] = held("x_pl1", [P, PACK - 1, PA], BF16)
        product(0)

        for i in range(TILES):
            if i == TILES - 2:
                for u in range(2):
                    quantise_x(0, u)
                for c in range(CHUNKS - 1):
                    quantise_page(0, c)
            scatter(i)
            if i + 1 == TILES:
                break
            round_page(i, 0, T2)
            product(i + 1)
            gather(i, 0, PA)
            if i == 1:
                late_w = held("trig2", [P, PASSES * KP], U32)
                late_sc = held("w1_sc1", [P, PASSES * KP], U8)
                nc.vector.quantize_mx(
                    out=late_w[:].bitcast(E4M3), scales=late_sc[:],
                    in_=late_bf[:].rearrange("p a t m j -> p (a t m j)"),
                )
                for a in range(PASSES):
                    w1_w[1, a] = late_w[:, a * KP : (a + 1) * KP]
                    w1_sc[1, a] = late_sc[:, a * KP : (a + 1) * KP]
                for n in range(PACK, TILES):
                    first_stage(n)
            if i == PACK - 1:
                weave_group(0)
            if i == TILES - 2:
                weave_group(1)
                quantise_page(0, CHUNKS - 1)
                for mt in range(T2 // P):
                    second_stage(0, mt)

        last = TILES - 1
        last_sign = held("page_pl1", [P, 1], F32)
        nc.scalar.copy(last_sign[:], sgn[:, GROUPS - 1, PACK - 1 : PACK])

        def last_x(u):
            picked = held("picked_last%d" % u, [P, CHUNK], F32)
            nc.vector.tensor_copy(picked[:], page[last][:].indirect(idx3[:, u * CHUNK // 16 : (u + 1) * CHUNK // 16]))
            nc.scalar.activation(
                x_bf[1, u][:, :, PACK - 1], picked[:], ACT.Abs, scale=anc[:, GROUPS - 1, PACK - 1 : PACK]
            )

        def last_page(c):
            nc.vector.tensor_scalar(
                page_bf[1, c][:, :, PACK - 1], page[last][:, c * CHUNK : (c + 1) * CHUNK], last_sign[:], None, ALU.mult
            )

        last_x(0)
        last_x(1)
        last_page(0)
        last_page(1)
        quantise_page(1, 0)
        quantise_x(1, 0)
        quantise_x(1, 1)
        last_page(2)
        quantise_page(1, 1)
        last_page(3)
        quantise_page(1, 2)
        quantise_page(1, 3)
        for mt in range(T2 // P):
            second_stage(1, mt)
            finish(mt, mt in (5, 7))
